import numpy as np
import ml_dtypes


def mxq(x, axis, fmt="e4m3"):
    dtype, down = {"e4m3": (ml_dtypes.float8_e4m3fn, 7), "e5m2": (ml_dtypes.float8_e5m2, 14)}[fmt]
    v = np.moveaxis(np.asarray(x, np.float32).astype(ml_dtypes.bfloat16).astype(np.float64), axis, -1)
    blocks = v.reshape(v.shape[:-1] + (-1, 32))
    amax = np.abs(blocks).max(-1, keepdims=True)
    byte = np.maximum(np.where(amax > 0, np.frexp(amax)[1] - 1 + 127, 0) - down, 1)
    scale = np.exp2(byte - 127.0)
    codes = (blocks / scale).astype(np.float32).astype(dtype).astype(np.float64)
    return np.moveaxis((codes * scale).reshape(v.shape), -1, axis)


WIDE = False


def mx_kscale(k):
    if not WIDE:
        return np.ones(k)
    levels = np.array([30, -30])
    if k % 512:
        return np.exp2(np.random.permutation(np.resize(levels, k // 32))).repeat(32)
    a = np.empty((k // 512, 16))
    for p in range(k // 512):
        a[p, :8] = np.random.permutation(np.resize(levels, 8))
        for g in range(8):
            far = levels[np.abs(levels - a[p, g]) >= 10]
            a[p, g + 8] = far[np.random.randint(len(far))]
    return np.exp2(a.ravel()).repeat(32)


BF16 = ml_dtypes.bfloat16


def bf(x):
    return np.asarray(x, np.float32).astype(BF16)


def f64(x):
    return np.asarray(x).astype(np.float64)


E2M1 = np.array([0.0, 0.5, 1.0, 1.5, 2.0, 3.0, 4.0, 6.0, -0.0, -0.5, -1.0, -1.5, -2.0, -3.0, -4.0, -6.0])


def pack_weight(w, fmt):
    k, n = w.shape
    w = f64(bf(w)).reshape(k // 32, 32, n)
    amax = np.abs(w).max(1)
    if fmt == "e4m3":
        byte = np.frexp(amax)[1] - 1 + 127 - 7
    else:
        mant, ex = np.frexp(amax / 6.0)
        byte = np.where(mant > 0.5, ex, ex - 1) + 127
    byte = np.clip(np.where(amax > 0, byte, 1), 1, 254)
    scaled = (w * np.exp2(127.0 - byte)[:, None, :]).reshape(k, n).astype(np.float32)
    by_word = np.ascontiguousarray(scaled.reshape(k // 512, 128, 4, n).transpose(0, 1, 3, 2))
    if fmt == "e4m3":
        words = by_word.astype(ml_dtypes.float8_e4m3fn).view(np.uint8)
    else:
        c = by_word.astype(ml_dtypes.float4_e2m1fn).view(np.uint8) & 0xF
        words = c[..., 0::2] | (c[..., 1::2] << 4)
    return np.ascontiguousarray(words), np.ascontiguousarray(byte.astype(np.uint8).reshape(k // 512, 16, n))


def unpack_weight(words, scales, fmt):
    g, p, n, _ = words.shape
    if fmt == "e4m3":
        vals = np.ascontiguousarray(words).view(ml_dtypes.float8_e4m3fn).astype(np.float64)
    else:
        nib = np.empty((g, p, n, 4), np.uint8)
        nib[..., 0::2] = words & 0xF
        nib[..., 1::2] = words >> 4
        vals = E2M1[nib]
    vals = vals * np.repeat(np.exp2(scales.astype(np.float64) - 127.0), 8, axis=1)[..., None]
    return vals.transpose(0, 1, 3, 2).reshape(g * 512, n)
def pack4(w):
    words, scales = pack_weight(w, "e2m1")
    return words.reshape(words.shape[0], 128, -1), scales


def unpack4(words, scales):
    return unpack_weight(words.reshape(words.shape[0], 128, -1, 2), scales, "e2m1")


M, K, F, D = 1024, 1024, 2048, 512


def setup_inputs():
    s, t = mx_kscale(K), mx_kscale(F)
    w = np.random.standard_normal((K, F)) / np.sqrt(K) / s[:, None] * t
    w_words, w_scales = pack4(w)
    share = np.square(np.random.standard_normal((F, D))) - 1.0
    return {"state": bf(np.random.standard_normal((M, K)) * s),
            "w_words": w_words,
            "w_scales": w_scales,
            "ref_loss": bf(0.5 * np.random.standard_normal(F) * t),
            "member": bf(0.5 * share / np.sqrt(F) / t[:, None]),
            "alpha": bf(np.exp(0.3 * np.random.standard_normal((M, D))))}


def reference(state, w_words, w_scales, ref_loss, member, alpha):
    loss = mxq(f64(state), 1, "e4m3") @ unpack4(w_words, w_scales)
    excess = np.maximum(loss - f64(ref_loss), 0.0)
    lam = mxq(excess, 1, "e5m2") @ mxq(f64(member), 0, "e4m3")
    grown = f64(alpha) * np.exp(lam)
    return grown / np.mean(grown, axis=1, keepdims=True)

@@ -1,0 +1,393 @@
+from contextlib import ExitStack
+
+import concourse.mybir as mybir
+from concourse.masks import make_identity
+
+M, K, F, D = 1024, 1024, 2048, 512
+FLOPS = 2 * M * K * F + 2 * M * F * D
+
+F32 = mybir.dt.float32
+BF16 = mybir.dt.bfloat16
+I32 = mybir.dt.int32
+U32 = mybir.dt.uint32
+U8 = mybir.dt.uint8
+E4M3X4 = mybir.dt.float8_e4m3fn_x4
+E5M2X4 = mybir.dt.float8_e5m2_x4
+E2M1X4 = mybir.dt.float4_e2m1fn_x4
+ACT = mybir.ActivationFunctionType
+ALU = mybir.AluOpType
+
+P = 128
+T = 4
+KG = K // 512
+FG = F // 512
+HALF = 512
+NH = M // HALF
+MT = HALF // P
+
+
+def tile_doremi_domain_reweighting_s9_kernel(
+    tc, state, w_words, w_scales, ref_loss, member, alpha, out
+):
+    nc = tc.nc
+    with ExitStack() as ctx:
+        keep = ctx.enter_context(tc.tile_pool(name="keep", bufs=1))
+        stage = ctx.enter_context(tc.tile_pool(name="stage", bufs=4))
+        psum = ctx.enter_context(tc.psum_pool(name="psum", bufs=1))
+
+        ident = keep.tile([P, P], F32, name="ident")
+        ws_raw = keep.tile([P, KG, F], U8, name="ws_raw", align_bytes=64)
+        ws = keep.tile([P, KG, T, F // T], U8, name="ws", align_bytes=64)
+        w_raw = keep.tile([P, KG, 2 * F], U8, name="w_raw", align_bytes=64)
+        w = keep.tile([P, KG, T, 2 * F // T], U8, name="w", align_bytes=64)
+        ref_rows = keep.tile([P, HALF], BF16, name="ref_rows")
+        minus = keep.tile([P, T], BF16, name="minus")
+        zeros = keep.tile([P, HALF], BF16, name="zeros")
+        negref = keep.tile([P, FG, T], F32, name="negref")
+        warm = keep.tile([P, 1], F32, name="warm")
+        warm_out = keep.tile([P, 1], F32, name="warm_out")
+        s_codes = [keep.tile([P, KG, HALF], U32, name="s_codes%d" % h, align_bytes=64) for h in range(NH)]
+        s_scales = [keep.tile([P, KG, HALF], U8, name="s_scales%d" % h, align_bytes=64) for h in range(NH)]
+        s_group = [keep.tile([P, KG, HALF, T], BF16, name="s_group%d" % h, align_bytes=64) for h in range(NH)]
+        x_codes = [keep.tile([P, FG, HALF], U32, name="x_codes%d" % h, align_bytes=64) for h in range(NH)]
+        x_scales = [keep.tile([P, FG, HALF], U8, name="x_scales%d" % h, align_bytes=64) for h in range(NH)]
+        m_codes = keep.tile([P, FG, D], U32, name="m_codes", align_bytes=64)
+        m_scales = keep.tile([P, FG, D], U8, name="m_scales", align_bytes=64)
+        s_raw = [keep.tile([P, K], BF16, name="s_raw%d" % c) for c in range(2 * MT)]
+        m_raw = [keep.tile([P, T, D], BF16, name="m_raw%d" % g) for g in range(FG)]
+        al = [keep.tile([P, MT, D], BF16, name="al%d" % h) for h in range(NH)]
+
+        def view(ap, pattern, **kw):
+            return ap.rearrange(pattern, **kw)
+
+        with tc.manual_schedule():
+            nc.vector.memset(ws_raw[:].bitcast(U32), 0)
+            nc.vector.memset(warm[:], 0.0)
+            nc.vector.memset(zeros[:], 0.0)
+            nc.vector.memset(ref_rows[:], 0.0)
+            make_identity(nc, ident[:])
+
+            def load_state(c):
+                nc.sync.dma_start(out=s_raw[c][:], in_=state[c * P : (c + 1) * P, :])
+
+            for c in range(MT):
+                load_state(c)
+            w_view = view(w_words, "g p n -> p g n")
+
+            def load_w(a, b):
+                nc.sync.dma_start(out=w_raw[:, :, a:b].bitcast(I32), in_=w_view[:, :, a:b].bitcast(I32))
+
+            load_w(0, 1024)
+
+            def load_scales(q, queue):
+                queue.dma_start(
+                    out=ws_raw[32 * q : 32 * q + 4, :, :].bitcast(I32),
+                    in_=view(w_scales[:, 4 * q : 4 * q + 4, :], "g r n -> r g n").bitcast(I32),
+                )
+
+            for q in range(3):
+                load_scales(q, nc.scalar)
+            load_scales(3, nc.gpsimd)
+            nc.gpsimd.dma_start(
+                out=view(ref_rows[0:T, :], "t (a r) -> t a r", r=8),
+                in_=view(ref_loss, "(a t r) -> t a r", t=T, r=8),
+            )
+            nc.scalar.activation(out=warm_out[:], in_=warm[:], func=ACT.Exp)
+            nc.vector.tensor_scalar(out=minus[:], in0=ident[:, 0:T], scalar1=-1.0, scalar2=None, op0=ALU.mult)
+            m_view = view(member, "(g b t r) d -> g t b r d", b=16, t=T, r=8)
+
+            def load_member(g):
+                for t in range(T):
+                    nc.sync.dma_start(out=m_raw[g][:, t, :], in_=m_view[g, t])
+
+            load_w(1024, 4096)
+            load_member(0)
+            for c in range(MT, 2 * MT):
+                load_state(c)
+            for g in range(1, FG):
+                load_member(g)
+            a_view = view(alpha, "(h i p) d -> h p i d", i=MT, p=P)
+            for h in range(NH):
+                nc.sync.dma_start(out=al[h][:], in_=a_view[h])
+
+            def dummy(n, tag):
+                for j in range(n):
+                    junk = psum.tile([P, HALF], F32, name="junk", tag=tag)
+                    nc.tensor.matmul(out=junk[:], lhsT=zeros[:, 0:P], rhs=zeros[:], start=True, stop=True)
+
+            def turn_state(c, bank):
+                xt = psum.tile([P, KG, 2, P], F32, name="xt%d" % c, tag=bank)
+                words = s_raw[c][:].bitcast(F32)
+                for g in range(KG):
+                    for u in range(2):
+                        nc.tensor.transpose(
+                            xt[:, g, u, :], words[:, 256 * g + u : 256 * (g + 1) : 2], ident[:]
+                        )
+                return xt
+
+            def copy_state(c, xt, eng):
+                h, i = divmod(c, MT)
+                dst = s_group[h][:].bitcast(F32)[:, :, i * P : (i + 1) * P, :]
+                src = view(xt[:], "p g u m -> p g m u")
+                if eng == "v":
+                    nc.vector.tensor_copy(out=dst, in_=src)
+                else:
+                    nc.scalar.copy(out=dst, in_=src)
+
+            def quant_state(h, g, a, b):
+                nc.vector.quantize_mx(
+                    out=s_codes[h][:, g, a:b].bitcast(E4M3X4),
+                    scales=s_scales[h][:, g, a:b],
+                    in_=view(s_group[h][:, g, a:b, :], "p m t -> p (m t)"),
+                )
+
+            def perm_w(g, a, b):
+                nc.vector.tensor_copy(
+                    out=view(w[:, g, :, 256 * a : 256 * b].bitcast(I32), "p t (b w) -> p t b w", w=4),
+                    in_=view(w_raw[:, g, 1024 * a : 1024 * b].bitcast(I32), "p (b t w) -> p t b w", t=T, w=4),
+                )
+
+            def perm_scales(g, a, b):
+                nc.vector.tensor_copy(
+                    out=view(ws[:, g, :, P * a : P * b].bitcast(I32), "p t (b w) -> p t b w", w=2),
+                    in_=view(ws_raw[:, g, 512 * a : 512 * b].bitcast(I32), "p (b t w) -> p t b w", t=T, w=2),
+                )
+
+            def stage1(h, g2, t):
+                bank = psum.tile([P, HALF], F32, name="loss_%d_%d_%d" % (h, g2, t), tag="A%d" % t)
+                for g in range(KG):
+                    nc.tensor.matmul_mx(
+                        out=bank[:],
+                        lhsT=w[:, g, t, 256 * g2 : 256 * (g2 + 1)].bitcast(E2M1X4),
+                        lhsT_scale=ws[:, g, t, P * g2 : P * (g2 + 1)],
+                        rhs=s_codes[h][:, g, :].bitcast(E4M3X4),
+                        rhs_scale=s_scales[h][:, g, :],
+                        start=(g == 0),
+                        stop=(g == KG - 1),
+                    )
+                return bank
+
+            def evac(e, bank, g2, t, eng):
+                if eng == "s":
+                    nc.scalar.activation(
+                        out=e[:, t, :], in_=bank[:], func=ACT.Relu, bias=negref[:, g2, t : t + 1], scale=1.0
+                    )
+                else:
+                    nc.vector.tensor_scalar(
+                        out=e[:, t, :], in0=bank[:], scalar1=negref[:, g2, t : t + 1], scalar2=0.0,
+                        op0=ALU.add, op1=ALU.max,
+                    )
+
+            def weave(dst, src, a, b):
+                nc.vector.tensor_copy(
+                    out=view(dst[:, a:b, :], "p (c i) t -> p c t i", i=4),
+                    in_=view(src[:, :, a:b], "p t (c i) -> p c t i", i=4),
+                )
+
+            def quant_x(h, g2, x, a, b):
+                nc.vector.quantize_mx(
+                    out=x_codes[h][:, g2, a:b].bitcast(E5M2X4),
+                    scales=x_scales[h][:, g2, a:b],
+                    in_=view(x[:, a:b, :], "p m t -> p (m t)"),
+                )
+
+            def quant_m(g2, x):
+                nc.vector.quantize_mx(
+                    out=m_codes[:, g2, :].bitcast(E4M3X4),
+                    scales=m_scales[:, g2, :],
+                    in_=view(x[:], "p m t -> p (m t)"),
+                )
+
+            def stage2(bank, h, i, g2):
+                nc.tensor.matmul_mx(
+                    out=bank[:],
+                    lhsT=x_codes[h][:, g2, i * P : (i + 1) * P].bitcast(E5M2X4),
+                    lhsT_scale=x_scales[h][:, g2, i * P : (i + 1) * P],
+                    rhs=m_codes[:, g2, :].bitcast(E4M3X4),
+                    rhs_scale=m_scales[:, g2, :],
+                    start=(g2 == 0),
+                    stop=(g2 == FG - 1),
+                )
+
+            def epi_exp(bank, h, i):
+                e = stage.tile([P, D], F32, name="e_%d_%d" % (h, i), tag="e", bufs=3)
+                nc.scalar.activation(out=e[:], in_=bank[:], func=ACT.Exp)
+                return e
+
+            def epi_mul(e, h, i):
+                grown = stage.tile([P, D], F32, name="grown_%d_%d" % (h, i), tag="grown", bufs=3)
+                total = stage.tile([P, 1], F32, name="total_%d_%d" % (h, i), tag="total", bufs=4)
+                nc.vector.scalar_tensor_tensor(
+                    out=grown[:], in0=e[:], scalar=1.0, in1=al[h][:, i, :], op0=ALU.mult, op1=ALU.mult,
+                    accum_out=total[:],
+                )
+                return grown, total
+
+            def epi_rec(total, h, i):
+                rec = stage.tile([P, 1], F32, name="rec_%d_%d" % (h, i), tag="rec", bufs=4)
+                nc.vector.reciprocal(out=rec[:], in_=total[:])
+                return rec
+
+            def epi_out(grown, rec, h, i, eng):
+                res = stage.tile([P, D], F32, name="res_%d_%d" % (h, i), tag="res", bufs=4)
+                if eng == "s":
+                    inv = stage.tile([P, 1], F32, name="inv_%d_%d" % (h, i), tag="inv", bufs=4)
+                    nc.gpsimd.tensor_scalar(out=inv[:], in0=rec[:], scalar1=float(D), scalar2=None, op0=ALU.mult)
+                    nc.scalar.activation(out=res[:], in_=grown[:], func=ACT.Copy, scale=inv[:])
+                else:
+                    nc.vector.tensor_scalar(
+                        out=res[:], in0=grown[:], scalar1=rec[:], scalar2=float(D), op0=ALU.mult, op1=ALU.mult
+                    )
+                row = h * HALF + i * P
+                nc.sync.dma_start(out=out[row : row + P, :], in_=res[:])
+
+            dummy(5, "A3")
+            xt = [None] * (2 * MT)
+            for c in range(MT):
+                xt[c] = turn_state(c, "B%d" % c)
+                copy_state(c, xt[c], "v" if c == 0 else "s")
+                if c == 1:
+                    for i in range(2):
+                        for g in range(KG):
+                            quant_state(0, g, P * i, P * (i + 1))
+            refT = psum.tile([P, FG, T], F32, name="refT", tag="A0")
+            for g2 in range(FG):
+                nc.tensor.matmul(
+                    out=refT[:, g2, :], lhsT=ref_rows[:, g2 * P : (g2 + 1) * P], rhs=minus[:],
+                    start=True, stop=True,
+                )
+            nc.scalar.copy(out=negref[:], in_=refT[:])
+            for g in range(KG):
+                perm_scales(g, 0, 1)
+            for g in range(KG):
+                perm_w(g, 0, 1)
+            for i in range(2, 4):
+                for g in range(KG):
+                    quant_state(0, g, P * i, P * (i + 1))
+            for g in range(KG):
+                perm_w(g, 1, FG)
+            for g in range(KG):
+                perm_scales(g, 1, FG)
+
+            exc = {}
+            xs = {}
+            mx = {}
+
+            def run_stage1(h, g2, engs="ssss"):
+                e = stage.tile([P, T, HALF], BF16, name="e_in_%d_%d" % (h, g2), tag="exc", bufs=5)
+                for t in range(T):
+                    bank = stage1(h, g2, t)
+                    evac(e, bank, g2, t, engs[t])
+                exc[h, g2] = e
+
+            def weave_x(h, g2):
+                x = stage.tile([P, HALF, T], BF16, name="x_%d_%d" % (h, g2), tag="x", bufs=2, align_bytes=64)
+                weave(x, exc[h, g2], 0, HALF)
+                xs[h, g2] = x
+
+            def weave_m(g2):
+                x = stage.tile([P, D, T], BF16, name="mx_%d" % g2, tag="mx", bufs=2, align_bytes=64)
+                weave(x, m_raw[g2], 0, D)
+                mx[g2] = x
+
+            def qx(h, g2):
+                quant_x(h, g2, xs[h, g2], 0, HALF)
+
+            def qm(g2):
+                quant_m(g2, mx[g2])
+
+            run_stage1(0, 0)
+            run_stage1(0, 1)
+            for c in range(MT, 2 * MT):
+                xt[c] = turn_state(c, "B%d" % (c - MT))
+                copy_state(c, xt[c], "s")
+            run_stage1(0, 2)
+            run_stage1(0, 3)
+            weave_m(0)
+            weave_x(0, 0)
+            qm(0)
+            qx(0, 0)
+            weave_m(1)
+            weave_x(0, 1)
+            for g in range(KG):
+                quant_state(1, g, 0, 512)
+            qm(1)
+            qx(0, 1)
+            weave_m(2)
+            weave_x(0, 2)
+            qm(2)
+            qx(0, 2)
+            weave_m(3)
+            weave_x(0, 3)
+            qm(3)
+            qx(0, 3)
+
+            done = {}
+            es = {}
+            recs = {}
+
+            def run_stage2(h, i, groups, bank=None):
+                if bank is None:
+                    bank = psum.tile([P, D], F32, name="lam_%d_%d" % (h, i), tag="B%d" % i)
+                for g2 in groups:
+                    stage2(bank, h, i, g2)
+                return bank
+
+            def exp(h, i, bank):
+                es[h, i] = epi_exp(bank, h, i)
+
+            def mul(h, i):
+                done[h, i] = epi_mul(es[h, i], h, i)
+
+            def rec(h, i):
+                recs[h, i] = epi_rec(done[h, i][1], h, i)
+
+            def fin(h, i, eng):
+                epi_out(done[h, i][0], recs[h, i], h, i, eng)
+
+            run_stage1(1, 0)
+            run_stage1(1, 1)
+            weave_x(1, 0)
+            weave_x(1, 1)
+            qx(1, 0)
+            qx(1, 1)
+            for i in range(2):
+                exp(0, i, run_stage2(0, i, range(FG)))
+            run_stage1(1, 2)
+            for i in range(2, 4):
+                exp(0, i, run_stage2(0, i, range(FG)))
+            mul(0, 0)
+            mul(0, 1)
+            rec(0, 0)
+            rec(0, 1)
+            weave_x(1, 2)
+            mul(0, 2)
+            qx(1, 2)
+            mul(0, 3)
+            rec(0, 2)
+            rec(0, 3)
+            run_stage1(1, 3, "ssss")
+            fin(0, 0, "s")
+            fin(0, 1, "s")
+            banks = {}
+            for i in range(4):
+                banks[i] = run_stage2(1, i, range(FG - 1))
+            x = stage.tile([P, HALF, T], BF16, name="x_1_3", tag="x", bufs=2, align_bytes=64)
+            last = exc[1, 3]
+            for i in range(4):
+                weave(x, last, i * P, (i + 1) * P)
+                if i:
+                    quant_x(1, 3, x, (i - 1) * P, i * P)
+            quant_x(1, 3, x, 3 * P, 4 * P)
+            fin(0, 2, "s")
+            fin(0, 3, "s")
+            for i in range(4):
+                run_stage2(1, i, [FG - 1], banks[i])
+                exp(1, i, banks[i])
+            for i in range(4):
+                mul(1, i)
+                if i:
+                    rec(1, i - 1)
+                    fin(1, i - 1, "s" if i == 1 else "v")
+            rec(1, 3)
+            fin(1, 3, "v")

@@ -44,6 +44,8 @@ def tile_doremi_domain_reweighting_s9_kernel(
         minus = keep.tile([P, T], BF16, name="minus")
         zeros = keep.tile([P, HALF], BF16, name="zeros")
         negref = keep.tile([P, FG, T], F32, name="negref")
+        totals = [keep.tile([P, MT], F32, name="totals%d" % h) for h in range(NH)]
+        inv = [keep.tile([P, MT], F32, name="inv%d" % h) for h in range(NH)]
         warm = keep.tile([P, 1], F32, name="warm")
         warm_out = keep.tile([P, 1], F32, name="warm_out")
         s_codes = [keep.tile([P, KG, HALF], U32, name="s_codes%d" % h, align_bytes=64) for h in range(NH)]
@@ -61,45 +63,46 @@ def tile_doremi_domain_reweighting_s9_kernel(
             return ap.rearrange(pattern, **kw)
 
         with tc.manual_schedule():
-            nc.vector.memset(ws_raw[:].bitcast(U32), 0)
-            nc.vector.memset(warm[:], 0.0)
-            nc.vector.memset(zeros[:], 0.0)
             nc.vector.memset(ref_rows[:], 0.0)
+            nc.vector.memset(ws_raw[:].bitcast(U32), 0)
+            nc.vector.memset(zeros[:], 0.0)
+            nc.vector.memset(warm[:], 0.0)
             make_identity(nc, ident[:])
 
             def load_state(c):
                 nc.sync.dma_start(out=s_raw[c][:], in_=state[c * P : (c + 1) * P, :])
 
-            for c in range(MT):
-                load_state(c)
+            def load_scales(q, a, b, queue):
+                queue.dma_start(
+                    out=ws_raw[32 * q : 32 * q + 4, :, a:b].bitcast(I32),
+                    in_=view(w_scales[:, 4 * q : 4 * q + 4, a:b], "g r n -> r g n").bitcast(I32),
+                )
+
             w_view = view(w_words, "g p n -> p g n")
 
             def load_w(a, b):
                 nc.sync.dma_start(out=w_raw[:, :, a:b].bitcast(I32), in_=w_view[:, :, a:b].bitcast(I32))
 
-            load_w(0, 1024)
-
-            def load_scales(q, queue):
-                queue.dma_start(
-                    out=ws_raw[32 * q : 32 * q + 4, :, :].bitcast(I32),
-                    in_=view(w_scales[:, 4 * q : 4 * q + 4, :], "g r n -> r g n").bitcast(I32),
-                )
-
-            for q in range(3):
-                load_scales(q, nc.scalar)
-            load_scales(3, nc.gpsimd)
-            nc.gpsimd.dma_start(
-                out=view(ref_rows[0:T, :], "t (a r) -> t a r", r=8),
-                in_=view(ref_loss, "(a t r) -> t a r", t=T, r=8),
-            )
-            nc.scalar.activation(out=warm_out[:], in_=warm[:], func=ACT.Exp)
-            nc.vector.tensor_scalar(out=minus[:], in0=ident[:, 0:T], scalar1=-1.0, scalar2=None, op0=ALU.mult)
             m_view = view(member, "(g b t r) d -> g t b r d", b=16, t=T, r=8)
 
             def load_member(g):
                 for t in range(T):
                     nc.sync.dma_start(out=m_raw[g][:, t, :], in_=m_view[g, t])
 
+            load_state(0)
+            nc.scalar.dma_start(
+                out=view(ref_rows[0:T, :], "t (a r) -> t a r", r=8),
+                in_=view(ref_loss, "(a t r) -> t a r", t=T, r=8),
+            )
+            for c in range(1, MT):
+                load_state(c)
+            for q in range(2):
+                load_scales(q, 0, F, nc.scalar)
+            for q in range(2, 4):
+                load_scales(q, 0, F, nc.gpsimd)
+            load_w(0, 1024)
+            nc.scalar.activation(out=warm_out[:], in_=warm[:], func=ACT.Exp)
+            nc.vector.tensor_scalar(out=minus[:], in0=ident[:, 0:T], scalar1=-1.0, scalar2=None, op0=ALU.mult)
             load_w(1024, 4096)
             load_member(0)
             for c in range(MT, 2 * MT):
@@ -210,38 +213,86 @@ def tile_doremi_domain_reweighting_s9_kernel(
                 )
 
             def epi_exp(bank, h, i):
-                e = stage.tile([P, D], F32, name="e_%d_%d" % (h, i), tag="e", bufs=3)
+                e = stage.tile([P, D], F32, name="e_%d_%d" % (h, i), tag="e", bufs=4)
                 nc.scalar.activation(out=e[:], in_=bank[:], func=ACT.Exp)
                 return e
 
             def epi_mul(e, h, i):
-                grown = stage.tile([P, D], F32, name="grown_%d_%d" % (h, i), tag="grown", bufs=3)
-                total = stage.tile([P, 1], F32, name="total_%d_%d" % (h, i), tag="total", bufs=4)
+                grown = stage.tile([P, D], F32, name="grown_%d_%d" % (h, i), tag="grown", bufs=6)
                 nc.vector.scalar_tensor_tensor(
                     out=grown[:], in0=e[:], scalar=1.0, in1=al[h][:, i, :], op0=ALU.mult, op1=ALU.mult,
-                    accum_out=total[:],
+                    accum_out=totals[h][:, i : i + 1],
                 )
-                return grown, total
+                return grown
 
-            def epi_rec(total, h, i):
-                rec = stage.tile([P, 1], F32, name="rec_%d_%d" % (h, i), tag="rec", bufs=4)
-                nc.vector.reciprocal(out=rec[:], in_=total[:])
-                return rec
+            def means(h, a, b):
+                nc.vector.tensor_scalar(
+                    out=totals[h][:, a:b], in0=totals[h][:, a:b], scalar1=1.0 / D, scalar2=None, op0=ALU.mult
+                )
 
-            def epi_out(grown, rec, h, i, eng):
-                res = stage.tile([P, D], F32, name="res_%d_%d" % (h, i), tag="res", bufs=4)
+            def invert(h, a, b):
+                nc.vector.reciprocal(out=inv[h][:, a:b], in_=totals[h][:, a:b])
+
+            def fin(h, i, eng):
+                res = stage.tile([P, D], F32, name="res_%d_%d" % (h, i), tag="res", bufs=8)
+                scale = inv[h][:, i : i + 1]
                 if eng == "s":
-                    inv = stage.tile([P, 1], F32, name="inv_%d_%d" % (h, i), tag="inv", bufs=4)
-                    nc.gpsimd.tensor_scalar(out=inv[:], in0=rec[:], scalar1=float(D), scalar2=None, op0=ALU.mult)
-                    nc.scalar.activation(out=res[:], in_=grown[:], func=ACT.Copy, scale=inv[:])
+                    nc.scalar.activation(out=res[:], in_=done[h, i][:], func=ACT.Copy, scale=scale)
                 else:
                     nc.vector.tensor_scalar(
-                        out=res[:], in0=grown[:], scalar1=rec[:], scalar2=float(D), op0=ALU.mult, op1=ALU.mult
+                        out=res[:], in0=done[h, i][:], scalar1=scale, scalar2=None, op0=ALU.mult
                     )
                 row = h * HALF + i * P
                 nc.sync.dma_start(out=out[row : row + P, :], in_=res[:])
 
-            dummy(5, "A3")
+            done = {}
+            es = {}
+            exc = {}
+            xs = {}
+            mx = {}
+
+            def run_stage1(h, g2, engs="ssss"):
+                e = stage.tile([P, T, HALF], BF16, name="e_in_%d_%d" % (h, g2), tag="exc", bufs=5)
+                for t in range(T):
+                    bank = stage1(h, g2, t)
+                    evac(e, bank, g2, t, engs[t])
+                exc[h, g2] = e
+
+            def weave_x(h, g2):
+                x = stage.tile([P, HALF, T], BF16, name="x_%d_%d" % (h, g2), tag="x", bufs=3, align_bytes=64)
+                weave(x, exc[h, g2], 0, HALF)
+                xs[h, g2] = x
+
+            def weave_m(g2):
+                x = stage.tile([P, D, T], BF16, name="mx_%d" % g2, tag="mx", bufs=2, align_bytes=64)
+                weave(x, m_raw[g2], 0, D)
+                mx[g2] = x
+
+            def qx(h, g2):
+                quant_x(h, g2, xs[h, g2], 0, HALF)
+
+            def qm(g2):
+                quant_m(g2, mx[g2])
+
+            lam = {}
+
+            def run_stage2(h, i, groups):
+                if (h, i) not in lam:
+                    lam[h, i] = psum.tile([P, D], F32, name="lam_%d_%d" % (h, i), tag="B%d" % i)
+                for g2 in groups:
+                    stage2(lam[h, i], h, i, g2)
+
+            def stage2_all(h, groups):
+                for i in range(MT):
+                    run_stage2(h, i, groups)
+
+            def exp(h, i):
+                es[h, i] = epi_exp(lam[h, i], h, i)
+
+            def mul(h, i):
+                done[h, i] = epi_mul(es[h, i], h, i)
+
+            dummy(4, "A3")
             xt = [None] * (2 * MT)
             for c in range(MT):
                 xt[c] = turn_state(c, "B%d" % c)
@@ -257,6 +308,7 @@ def tile_doremi_domain_reweighting_s9_kernel(
                     start=True, stop=True,
                 )
             nc.scalar.copy(out=negref[:], in_=refT[:])
+            dummy(3, "A3")
             for g in range(KG):
                 perm_scales(g, 0, 1)
             for g in range(KG):
@@ -268,34 +320,6 @@ def tile_doremi_domain_reweighting_s9_kernel(
                 perm_w(g, 1, FG)
             for g in range(KG):
                 perm_scales(g, 1, FG)
-
-            exc = {}
-            xs = {}
-            mx = {}
-
-            def run_stage1(h, g2, engs="ssss"):
-                e = stage.tile([P, T, HALF], BF16, name="e_in_%d_%d" % (h, g2), tag="exc", bufs=5)
-                for t in range(T):
-                    bank = stage1(h, g2, t)
-                    evac(e, bank, g2, t, engs[t])
-                exc[h, g2] = e
-
-            def weave_x(h, g2):
-                x = stage.tile([P, HALF, T], BF16, name="x_%d_%d" % (h, g2), tag="x", bufs=2, align_bytes=64)
-                weave(x, exc[h, g2], 0, HALF)
-                xs[h, g2] = x
-
-            def weave_m(g2):
-                x = stage.tile([P, D, T], BF16, name="mx_%d" % g2, tag="mx", bufs=2, align_bytes=64)
-                weave(x, m_raw[g2], 0, D)
-                mx[g2] = x
-
-            def qx(h, g2):
-                quant_x(h, g2, xs[h, g2], 0, HALF)
-
-            def qm(g2):
-                quant_m(g2, mx[g2])
-
             run_stage1(0, 0)
             run_stage1(0, 1)
             for c in range(MT, 2 * MT):
@@ -307,87 +331,78 @@ def tile_doremi_domain_reweighting_s9_kernel(
             weave_x(0, 0)
             qm(0)
             qx(0, 0)
-            weave_m(1)
+            stage2_all(0, [0])
             weave_x(0, 1)
+            weave_m(1)
+            qx(0, 1)
             for g in range(KG):
                 quant_state(1, g, 0, 512)
             qm(1)
-            qx(0, 1)
-            weave_m(2)
-            weave_x(0, 2)
-            qm(2)
-            qx(0, 2)
-            weave_m(3)
-            weave_x(0, 3)
-            qm(3)
-            qx(0, 3)
-
-            done = {}
-            es = {}
-            recs = {}
-
-            def run_stage2(h, i, groups, bank=None):
-                if bank is None:
-                    bank = psum.tile([P, D], F32, name="lam_%d_%d" % (h, i), tag="B%d" % i)
-                for g2 in groups:
-                    stage2(bank, h, i, g2)
-                return bank
-
-            def exp(h, i, bank):
-                es[h, i] = epi_exp(bank, h, i)
-
-            def mul(h, i):
-                done[h, i] = epi_mul(es[h, i], h, i)
-
-            def rec(h, i):
-                recs[h, i] = epi_rec(done[h, i][1], h, i)
-
-            def fin(h, i, eng):
-                epi_out(done[h, i][0], recs[h, i], h, i, eng)
-
             run_stage1(1, 0)
+            stage2_all(0, [1])
+            weave_x(0, 2)
+            weave_m(2)
+            qx(0, 2)
+            qm(2)
             run_stage1(1, 1)
+            stage2_all(0, [2])
+            weave_x(0, 3)
+            weave_m(3)
+            qx(0, 3)
+            qm(3)
+            run_stage1(1, 2)
+            stage2_all(0, [3])
             weave_x(1, 0)
             weave_x(1, 1)
             qx(1, 0)
             qx(1, 1)
-            for i in range(2):
-                exp(0, i, run_stage2(0, i, range(FG)))
-            run_stage1(1, 2)
-            for i in range(2, 4):
-                exp(0, i, run_stage2(0, i, range(FG)))
-            mul(0, 0)
-            mul(0, 1)
-            rec(0, 0)
-            rec(0, 1)
+            for i in range(MT):
+                exp(0, i)
+            run_stage1(1, 3)
             weave_x(1, 2)
-            mul(0, 2)
+            mul(0, 0)
             qx(1, 2)
+            mul(0, 1)
+            mul(0, 2)
+            means(0, 0, 2)
             mul(0, 3)
-            rec(0, 2)
-            rec(0, 3)
-            run_stage1(1, 3, "ssss")
+            invert(0, 0, 2)
+            means(0, 2, 4)
+            x = stage.tile([P, HALF, T], BF16, name="x_1_3", tag="x", bufs=3, align_bytes=64)
+            last = exc[1, 3]
+            stage2_all(1, [0, 1, 2])
+
+            def piece(i):
+                weave(x, last, i * P, (i + 1) * P)
+
+            def qpiece(i):
+                quant_x(1, 3, x, i * P, (i + 1) * P)
+
+            piece(0)
+            invert(0, 2, 4)
+            piece(1)
+            qpiece(0)
             fin(0, 0, "s")
             fin(0, 1, "s")
-            banks = {}
-            for i in range(4):
-                banks[i] = run_stage2(1, i, range(FG - 1))
-            x = stage.tile([P, HALF, T], BF16, name="x_1_3", tag="x", bufs=2, align_bytes=64)
-            last = exc[1, 3]
-            for i in range(4):
-                weave(x, last, i * P, (i + 1) * P)
-                if i:
-                    quant_x(1, 3, x, (i - 1) * P, i * P)
-            quant_x(1, 3, x, 3 * P, 4 * P)
-            fin(0, 2, "s")
-            fin(0, 3, "s")
-            for i in range(4):
-                run_stage2(1, i, [FG - 1], banks[i])
-                exp(1, i, banks[i])
-            for i in range(4):
-                mul(1, i)
-                if i:
-                    rec(1, i - 1)
-                    fin(1, i - 1, "s" if i == 1 else "v")
-            rec(1, 3)
-            fin(1, 3, "v")
+            piece(2)
+            qpiece(1)
+            piece(3)
+            qpiece(2)
+            qpiece(3)
+            fin(0, 2, "v")
+            fin(0, 3, "v")
+            for i in range(MT):
+                run_stage2(1, i, [3])
+                exp(1, i)
+            mul(1, 0)
+            mul(1, 1)
+            means(1, 0, 2)
+            mul(1, 2)
+            invert(1, 0, 2)
+            mul(1, 3)
+            means(1, 2, 4)
+            fin(1, 0, "s")
+            fin(1, 1, "s")
+            invert(1, 2, 4)
+            fin(1, 2, "v")
+            fin(1, 3, "s")

@@ -19,6 +19,8 @@ ALU = mybir.AluOpType
 
 P = 128
 T = 4
+STATE_LOADS = ((0, 1), (1, 1), (2, 2), (4, 2), (6, 2))
+RUN = 2
 KG = K // 512
 FG = F // 512
 HALF = 512
@@ -42,7 +44,7 @@ def tile_doremi_domain_reweighting_s9_kernel(
         w = keep.tile([P, KG, T, 2 * F // T], U8, name="w", align_bytes=64)
         ref_rows = keep.tile([P, HALF], BF16, name="ref_rows")
         minus = keep.tile([P, T], BF16, name="minus")
-        zeros = keep.tile([P, HALF], BF16, name="zeros")
+        zeros = keep.tile([P, HALF // 2], I32, name="zeros")
         negref = keep.tile([P, FG, T], F32, name="negref")
         totals = [keep.tile([P, MT], F32, name="totals%d" % h) for h in range(NH)]
         inv = [keep.tile([P, MT], F32, name="inv%d" % h) for h in range(NH)]
@@ -55,7 +57,9 @@ def tile_doremi_domain_reweighting_s9_kernel(
         x_scales = [keep.tile([P, FG, HALF], U8, name="x_scales%d" % h, align_bytes=64) for h in range(NH)]
         m_codes = keep.tile([P, FG, D], U32, name="m_codes", align_bytes=64)
         m_scales = keep.tile([P, FG, D], U8, name="m_scales", align_bytes=64)
-        s_raw = [keep.tile([P, K], BF16, name="s_raw%d" % c) for c in range(2 * MT)]
+        s_raw = [
+            keep.tile([P, n, K], BF16, name="s_raw%d" % j) for j, (first, n) in enumerate(STATE_LOADS)
+        ]
         m_raw = [keep.tile([P, T, D], BF16, name="m_raw%d" % g) for g in range(FG)]
         al = [keep.tile([P, MT, D], BF16, name="al%d" % h) for h in range(NH)]
 
@@ -63,19 +67,17 @@ def tile_doremi_domain_reweighting_s9_kernel(
             return ap.rearrange(pattern, **kw)
 
         with tc.manual_schedule():
-            nc.vector.memset(ref_rows[:], 0.0)
-            nc.vector.memset(ws_raw[:].bitcast(U32), 0)
-            nc.vector.memset(zeros[:], 0.0)
+            nc.gpsimd.memset(ws_raw[:].bitcast(I32), 0)
+            nc.vector.memset(zeros[:], 0)
+            nc.vector.memset(ref_rows[:].bitcast(I32), 0)
             nc.vector.memset(warm[:], 0.0)
             make_identity(nc, ident[:])
 
-            def load_state(c):
-                nc.sync.dma_start(out=s_raw[c][:], in_=state[c * P : (c + 1) * P, :])
-
-            def load_scales(q, a, b, queue):
-                queue.dma_start(
-                    out=ws_raw[32 * q : 32 * q + 4, :, a:b].bitcast(I32),
-                    in_=view(w_scales[:, 4 * q : 4 * q + 4, a:b], "g r n -> r g n").bitcast(I32),
+            def load_state(j):
+                first, n = STATE_LOADS[j]
+                nc.sync.dma_start(
+                    out=s_raw[j][:],
+                    in_=view(state[first * P : (first + n) * P, :], "(i p) k -> p i k", p=P),
                 )
 
             w_view = view(w_words, "g p n -> p g n")
@@ -83,44 +85,52 @@ def tile_doremi_domain_reweighting_s9_kernel(
             def load_w(a, b):
                 nc.sync.dma_start(out=w_raw[:, :, a:b].bitcast(I32), in_=w_view[:, :, a:b].bitcast(I32))
 
+            def load_scales(q, a, b, queue):
+                queue.dma_start(
+                    out=ws_raw[32 * q : 32 * q + 4, :, a:b].bitcast(I32),
+                    in_=view(w_scales[:, 4 * q : 4 * q + 4, a:b], "g r n -> r g n").bitcast(I32),
+                )
+
             m_view = view(member, "(g b t r) d -> g t b r d", b=16, t=T, r=8)
 
             def load_member(g):
                 for t in range(T):
                     nc.sync.dma_start(out=m_raw[g][:, t, :], in_=m_view[g, t])
 
-            load_state(0)
-            nc.scalar.dma_start(
+            a_view = view(alpha, "(h i p) d -> h p i d", i=MT, p=P)
+
+            def load_alpha(h):
+                nc.sync.dma_start(out=al[h][:], in_=a_view[h])
+
+            for j in range(3):
+                load_state(j)
+            nc.sync.dma_start(
                 out=view(ref_rows[0:T, :], "t (a r) -> t a r", r=8),
                 in_=view(ref_loss, "(a t r) -> t a r", t=T, r=8),
             )
-            for c in range(1, MT):
-                load_state(c)
-            for q in range(2):
-                load_scales(q, 0, F, nc.scalar)
-            for q in range(2, 4):
-                load_scales(q, 0, F, nc.gpsimd)
+            for q in range(4):
+                load_scales(q, 0, F, nc.scalar if q < 3 else nc.sync)
             load_w(0, 1024)
             nc.scalar.activation(out=warm_out[:], in_=warm[:], func=ACT.Exp)
             nc.vector.tensor_scalar(out=minus[:], in0=ident[:, 0:T], scalar1=-1.0, scalar2=None, op0=ALU.mult)
             load_w(1024, 4096)
             load_member(0)
-            for c in range(MT, 2 * MT):
-                load_state(c)
+            for j in range(3, 5):
+                load_state(j)
             for g in range(1, FG):
                 load_member(g)
-            a_view = view(alpha, "(h i p) d -> h p i d", i=MT, p=P)
             for h in range(NH):
-                nc.sync.dma_start(out=al[h][:], in_=a_view[h])
+                load_alpha(h)
 
-            def dummy(n, tag):
+            def dummy(n):
                 for j in range(n):
-                    junk = psum.tile([P, HALF], F32, name="junk", tag=tag)
-                    nc.tensor.matmul(out=junk[:], lhsT=zeros[:, 0:P], rhs=zeros[:], start=True, stop=True)
+                    junk = psum.tile([P, HALF], F32, name="junk", tag="A3")
+                    nc.tensor.matmul(out=junk[:], lhsT=zeros[:, 0:P].bitcast(BF16)[:, 0:P], rhs=zeros[:].bitcast(BF16), start=True, stop=True)
 
             def turn_state(c, bank):
                 xt = psum.tile([P, KG, 2, P], F32, name="xt%d" % c, tag=bank)
-                words = s_raw[c][:].bitcast(F32)
+                j = max(j for j in range(len(STATE_LOADS)) if STATE_LOADS[j][0] <= c)
+                words = s_raw[j][:, c - STATE_LOADS[j][0], :].bitcast(F32)
                 for g in range(KG):
                     for u in range(2):
                         nc.tensor.transpose(
@@ -170,6 +180,28 @@ def tile_doremi_domain_reweighting_s9_kernel(
                     )
                 return bank
 
+            def stage1_slice(h, g2, i):
+                bank = psum.tile([P, T, P], F32, name="slice_%d_%d_%d" % (h, g2, i), tag="A%d" % i)
+                for t in range(T):
+                    for g in range(KG):
+                        nc.tensor.matmul_mx(
+                            out=bank[:, t, :],
+                            lhsT=w[:, g, t, 256 * g2 : 256 * (g2 + 1)].bitcast(E2M1X4),
+                            lhsT_scale=ws[:, g, t, P * g2 : P * (g2 + 1)],
+                            rhs=s_codes[h][:, g, i * P : (i + 1) * P].bitcast(E4M3X4),
+                            rhs_scale=s_scales[h][:, g, i * P : (i + 1) * P],
+                            start=(g == 0),
+                            stop=(g == KG - 1),
+                        )
+                return bank
+
+            def evac_slice(e, bank, g2, i):
+                for t in range(T):
+                    nc.scalar.activation(
+                        out=e[:, t, i * P : (i + 1) * P], in_=bank[:, t, :], func=ACT.Relu,
+                        bias=negref[:, g2, t : t + 1], scale=1.0,
+                    )
+
             def evac(e, bank, g2, t, eng):
                 if eng == "s":
                     nc.scalar.activation(
@@ -183,8 +215,8 @@ def tile_doremi_domain_reweighting_s9_kernel(
 
             def weave(dst, src, a, b):
                 nc.vector.tensor_copy(
-                    out=view(dst[:, a:b, :], "p (c i) t -> p c t i", i=4),
-                    in_=view(src[:, :, a:b], "p t (c i) -> p c t i", i=4),
+                    out=view(dst[:, a:b, :], "p (c i) t -> p c t i", i=RUN),
+                    in_=view(src[:, :, a:b], "p t (c i) -> p c t i", i=RUN),
                 )
 
             def quant_x(h, g2, x, a, b):
@@ -292,35 +324,51 @@ def tile_doremi_domain_reweighting_s9_kernel(
             def mul(h, i):
                 done[h, i] = epi_mul(es[h, i], h, i)
 
-            dummy(4, "A3")
+            def new_exc(h, g2):
+                exc[h, g2] = stage.tile([P, T, HALF], BF16, name="e_in_%d_%d" % (h, g2), tag="exc", bufs=5)
+
+            def qs(i):
+                for g in range(KG):
+                    quant_state(0, g, P * i, P * (i + 1))
+
+            def slice0(i):
+                bank = stage1_slice(0, 0, i)
+                evac_slice(exc[0, 0], bank, 0, i)
+
+            dummy(5)
             xt = [None] * (2 * MT)
-            for c in range(MT):
-                xt[c] = turn_state(c, "B%d" % c)
-                copy_state(c, xt[c], "v" if c == 0 else "s")
-                if c == 1:
-                    for i in range(2):
-                        for g in range(KG):
-                            quant_state(0, g, P * i, P * (i + 1))
-            refT = psum.tile([P, FG, T], F32, name="refT", tag="A0")
+            new_exc(0, 0)
+            xt[0] = turn_state(0, "B0")
+            copy_state(0, xt[0], "v")
+            xt[1] = turn_state(1, "B1")
+            copy_state(1, xt[1], "s")
+            qs(0)
+            for g in range(KG):
+                perm_scales(g, 0, 1)
+            qs(1)
+            xt[2] = turn_state(2, "B2")
+            copy_state(2, xt[2], "s")
+            for g in range(KG):
+                perm_w(g, 0, 1)
+            xt[3] = turn_state(3, "B3")
+            copy_state(3, xt[3], "v")
+            refT = psum.tile([P, FG, T], F32, name="refT", tag="A3")
             for g2 in range(FG):
                 nc.tensor.matmul(
                     out=refT[:, g2, :], lhsT=ref_rows[:, g2 * P : (g2 + 1) * P], rhs=minus[:],
                     start=True, stop=True,
                 )
             nc.scalar.copy(out=negref[:], in_=refT[:])
-            dummy(3, "A3")
-            for g in range(KG):
-                perm_scales(g, 0, 1)
-            for g in range(KG):
-                perm_w(g, 0, 1)
-            for i in range(2, 4):
-                for g in range(KG):
-                    quant_state(0, g, P * i, P * (i + 1))
+            slice0(0)
+            slice0(1)
+            qs(2)
+            qs(3)
+            slice0(2)
+            slice0(3)
             for g in range(KG):
                 perm_w(g, 1, FG)
             for g in range(KG):
                 perm_scales(g, 1, FG)
-            run_stage1(0, 0)
             run_stage1(0, 1)
             for c in range(MT, 2 * MT):
                 xt[c] = turn_state(c, "B%d" % (c - MT))

@@ -42,10 +42,13 @@ def tile_doremi_domain_reweighting_s9_kernel(
         ws = keep.tile([P, KG, T, F // T], U8, name="ws", align_bytes=64)
         w_raw = keep.tile([P, KG, 2 * F], U8, name="w_raw", align_bytes=64)
         w = keep.tile([P, KG, T, 2 * F // T], U8, name="w", align_bytes=64)
-        ref_rows = keep.tile([P, HALF], BF16, name="ref_rows")
-        minus = keep.tile([P, T], BF16, name="minus")
-        zeros = keep.tile([P, HALF // 2], I32, name="zeros")
-        negref = keep.tile([P, FG, T], F32, name="negref")
+        ref_rows = keep.tile([P, P], BF16, name="ref_rows")
+        ref_wide = keep.tile([P, T, 4, 4, 8], BF16, name="ref_wide")
+        row_mod = keep.tile([P, 4], F32, name="row_mod")
+        row_div = keep.tile([P, FG], F32, name="row_div")
+        minus = keep.tile([P, FG], BF16, name="minus")
+        zeros = keep.tile([P, HALF], BF16, name="zeros")
+        negref = keep.tile([P, T, FG], F32, name="negref")
         totals = [keep.tile([P, MT], F32, name="totals%d" % h) for h in range(NH)]
         inv = [keep.tile([P, MT], F32, name="inv%d" % h) for h in range(NH)]
         warm = keep.tile([P, 1], F32, name="warm")
@@ -67,9 +70,10 @@ def tile_doremi_domain_reweighting_s9_kernel(
             return ap.rearrange(pattern, **kw)
 
         with tc.manual_schedule():
-            nc.gpsimd.memset(ws_raw[:].bitcast(I32), 0)
-            nc.vector.memset(zeros[:], 0)
+            nc.gpsimd.memset(ws_raw[:, 1, :].bitcast(I32), 0)
+            nc.vector.memset(ws_raw[:, 0, :].bitcast(I32), 0)
             nc.vector.memset(ref_rows[:].bitcast(I32), 0)
+            nc.vector.memset(zeros[:].bitcast(I32), 0)
             nc.vector.memset(warm[:], 0.0)
             make_identity(nc, ident[:])
 
@@ -85,10 +89,10 @@ def tile_doremi_domain_reweighting_s9_kernel(
             def load_w(a, b):
                 nc.sync.dma_start(out=w_raw[:, :, a:b].bitcast(I32), in_=w_view[:, :, a:b].bitcast(I32))
 
-            def load_scales(q, a, b, queue):
-                queue.dma_start(
-                    out=ws_raw[32 * q : 32 * q + 4, :, a:b].bitcast(I32),
-                    in_=view(w_scales[:, 4 * q : 4 * q + 4, a:b], "g r n -> r g n").bitcast(I32),
+            def load_scales(q):
+                nc.sync.dma_start(
+                    out=ws_raw[32 * q : 32 * q + 4, :, :].bitcast(I32),
+                    in_=view(w_scales[:, 4 * q : 4 * q + 4, :], "g r n -> r g n").bitcast(I32),
                 )
 
             m_view = view(member, "(g b t r) d -> g t b r d", b=16, t=T, r=8)
@@ -102,17 +106,14 @@ def tile_doremi_domain_reweighting_s9_kernel(
             def load_alpha(h):
                 nc.sync.dma_start(out=al[h][:], in_=a_view[h])
 
-            for j in range(3):
-                load_state(j)
-            nc.sync.dma_start(
-                out=view(ref_rows[0:T, :], "t (a r) -> t a r", r=8),
-                in_=view(ref_loss, "(a t r) -> t a r", t=T, r=8),
-            )
-            for q in range(4):
-                load_scales(q, 0, F, nc.scalar if q < 3 else nc.sync)
-            load_w(0, 1024)
             nc.scalar.activation(out=warm_out[:], in_=warm[:], func=ACT.Exp)
-            nc.vector.tensor_scalar(out=minus[:], in0=ident[:, 0:T], scalar1=-1.0, scalar2=None, op0=ALU.mult)
+            load_state(0)
+            load_state(1)
+            for q in range(4):
+                load_scales(q)
+            nc.sync.dma_start(out=ref_rows[0 : F // P, :], in_=view(ref_loss, "(c j) -> c j", j=P))
+            load_state(2)
+            load_w(0, 1024)
             load_w(1024, 4096)
             load_member(0)
             for j in range(3, 5):
@@ -125,7 +126,7 @@ def tile_doremi_domain_reweighting_s9_kernel(
             def dummy(n):
                 for j in range(n):
                     junk = psum.tile([P, HALF], F32, name="junk", tag="A3")
-                    nc.tensor.matmul(out=junk[:], lhsT=zeros[:, 0:P].bitcast(BF16)[:, 0:P], rhs=zeros[:].bitcast(BF16), start=True, stop=True)
+                    nc.tensor.matmul(out=junk[:], lhsT=zeros[:, 0:P], rhs=zeros[:], start=True, stop=True)
 
             def turn_state(c, bank):
                 xt = psum.tile([P, KG, 2, P], F32, name="xt%d" % c, tag=bank)
@@ -199,22 +200,28 @@ def tile_doremi_domain_reweighting_s9_kernel(
                 for t in range(T):
                     nc.scalar.activation(
                         out=e[:, t, i * P : (i + 1) * P], in_=bank[:, t, :], func=ACT.Relu,
-                        bias=negref[:, g2, t : t + 1], scale=1.0,
+                        bias=negref[:, t, g2 : g2 + 1], scale=1.0,
                     )
 
             def evac(e, bank, g2, t, eng):
                 if eng == "s":
                     nc.scalar.activation(
-                        out=e[:, t, :], in_=bank[:], func=ACT.Relu, bias=negref[:, g2, t : t + 1], scale=1.0
+                        out=e[:, t, :], in_=bank[:], func=ACT.Relu, bias=negref[:, t, g2 : g2 + 1], scale=1.0
                     )
                 else:
                     nc.vector.tensor_scalar(
-                        out=e[:, t, :], in0=bank[:], scalar1=negref[:, g2, t : t + 1], scalar2=0.0,
+                        out=e[:, t, :], in0=bank[:], scalar1=negref[:, t, g2 : g2 + 1], scalar2=0.0,
                         op0=ALU.add, op1=ALU.max,
                     )
 
             def weave(dst, src, a, b):
                 nc.vector.tensor_copy(
+                    out=view(dst[:, a:b, :], "p (c i) t -> p c t i", i=RUN),
+                    in_=view(src[:, :, a:b], "p t (c i) -> p c t i", i=RUN),
+                )
+
+            def weave_s(dst, src, a, b):
+                nc.scalar.copy(
                     out=view(dst[:, a:b, :], "p (c i) t -> p c t i", i=RUN),
                     in_=view(src[:, :, a:b], "p t (c i) -> p c t i", i=RUN),
                 )
@@ -245,12 +252,12 @@ def tile_doremi_domain_reweighting_s9_kernel(
                 )
 
             def epi_exp(bank, h, i):
-                e = stage.tile([P, D], F32, name="e_%d_%d" % (h, i), tag="e", bufs=4)
+                e = stage.tile([P, D], F32, name="e_%d_%d" % (h, i), tag="e", bufs=8)
                 nc.scalar.activation(out=e[:], in_=bank[:], func=ACT.Exp)
                 return e
 
             def epi_mul(e, h, i):
-                grown = stage.tile([P, D], F32, name="grown_%d_%d" % (h, i), tag="grown", bufs=6)
+                grown = stage.tile([P, D], F32, name="grown_%d_%d" % (h, i), tag="grown", bufs=8)
                 nc.vector.scalar_tensor_tensor(
                     out=grown[:], in0=e[:], scalar=1.0, in1=al[h][:, i, :], op0=ALU.mult, op1=ALU.mult,
                     accum_out=totals[h][:, i : i + 1],
@@ -270,6 +277,10 @@ def tile_doremi_domain_reweighting_s9_kernel(
                 scale = inv[h][:, i : i + 1]
                 if eng == "s":
                     nc.scalar.activation(out=res[:], in_=done[h, i][:], func=ACT.Copy, scale=scale)
+                elif eng == "v2":
+                    nc.vector.tensor_scalar(
+                        out=res[:], in0=done[h, i][:], scalar1=scale, scalar2=float(D), op0=ALU.mult, op1=ALU.mult
+                    )
                 else:
                     nc.vector.tensor_scalar(
                         out=res[:], in0=done[h, i][:], scalar1=scale, scalar2=None, op0=ALU.mult
@@ -295,10 +306,11 @@ def tile_doremi_domain_reweighting_s9_kernel(
                 weave(x, exc[h, g2], 0, HALF)
                 xs[h, g2] = x
 
-            def weave_m(g2):
-                x = stage.tile([P, D, T], BF16, name="mx_%d" % g2, tag="mx", bufs=2, align_bytes=64)
-                weave(x, m_raw[g2], 0, D)
-                mx[g2] = x
+            def new_m(g2):
+                mx[g2] = stage.tile([P, D, T], BF16, name="mx_%d" % g2, tag="mx", bufs=3, align_bytes=64)
+
+            def weave_m(g2, a=0, b=D):
+                weave(mx[g2], m_raw[g2], a, b)
 
             def qx(h, g2):
                 quant_x(h, g2, xs[h, g2], 0, HALF)
@@ -335,30 +347,46 @@ def tile_doremi_domain_reweighting_s9_kernel(
                 bank = stage1_slice(0, 0, i)
                 evac_slice(exc[0, 0], bank, 0, i)
 
+            def slice1(i):
+                bank = stage1_slice(1, 3, i)
+                evac_slice(exc[1, 3], bank, 3, i)
+
             dummy(5)
+            nc.vector.tensor_reduce(
+                out=row_mod[:], in_=view(ident[:, 0:16], "p (a q) -> p q a", q=4), axis=mybir.AxisListType.X, op=ALU.add
+            )
+            nc.vector.tensor_reduce(
+                out=row_div[:], in_=view(ident[:, 0:16], "p (a q) -> p a q", q=4), axis=mybir.AxisListType.X, op=ALU.add
+            )
+            nc.vector.tensor_scalar(out=minus[:], in0=row_div[:], scalar1=-1.0, scalar2=None, op0=ALU.mult)
+            for q in range(4):
+                nc.vector.tensor_scalar(
+                    out=ref_wide[:, :, q, :, :], in0=view(ref_rows[:], "p (j t r) -> p t j r", j=4, t=T),
+                    scalar1=row_mod[:, q : q + 1], scalar2=None, op0=ALU.mult,
+                )
             xt = [None] * (2 * MT)
             new_exc(0, 0)
             xt[0] = turn_state(0, "B0")
             copy_state(0, xt[0], "v")
             xt[1] = turn_state(1, "B1")
+            refT = psum.tile([P, T, FG], F32, name="refT", tag="A3")
+            for t in range(T):
+                nc.tensor.matmul(
+                    out=refT[:, t, :], lhsT=view(ref_wide[:, t, :, :, :], "p q j r -> p (q j r)"), rhs=minus[:],
+                    start=True, stop=True,
+                )
             copy_state(1, xt[1], "s")
-            qs(0)
+            nc.scalar.copy(out=negref[:], in_=refT[:])
             for g in range(KG):
                 perm_scales(g, 0, 1)
+            qs(0)
             qs(1)
             xt[2] = turn_state(2, "B2")
             copy_state(2, xt[2], "s")
             for g in range(KG):
                 perm_w(g, 0, 1)
             xt[3] = turn_state(3, "B3")
-            copy_state(3, xt[3], "v")
-            refT = psum.tile([P, FG, T], F32, name="refT", tag="A3")
-            for g2 in range(FG):
-                nc.tensor.matmul(
-                    out=refT[:, g2, :], lhsT=ref_rows[:, g2 * P : (g2 + 1) * P], rhs=minus[:],
-                    start=True, stop=True,
-                )
-            nc.scalar.copy(out=negref[:], in_=refT[:])
+            copy_state(3, xt[3], "s")
             slice0(0)
             slice0(1)
             qs(2)
@@ -375,6 +403,8 @@ def tile_doremi_domain_reweighting_s9_kernel(
                 copy_state(c, xt[c], "s")
             run_stage1(0, 2)
             run_stage1(0, 3)
+            for g2 in range(FG):
+                new_m(g2)
             weave_m(0)
             weave_x(0, 0)
             qm(0)
@@ -448,9 +478,8 @@ def tile_doremi_domain_reweighting_s9_kernel(
             mul(1, 2)
             invert(1, 0, 2)
             mul(1, 3)
-            means(1, 2, 4)
             fin(1, 0, "s")
             fin(1, 1, "s")
             invert(1, 2, 4)
-            fin(1, 2, "v")
-            fin(1, 3, "s")
+            fin(1, 2, "v2")
+            fin(1, 3, "v2")

from contextlib import ExitStack

import concourse.mybir as mybir
from concourse.masks import make_identity

M, K, F, D = 1024, 1024, 2048, 512
FLOPS = 2 * M * K * F + 2 * M * F * D

F32 = mybir.dt.float32
BF16 = mybir.dt.bfloat16
I32 = mybir.dt.int32
U32 = mybir.dt.uint32
U8 = mybir.dt.uint8
E4M3X4 = mybir.dt.float8_e4m3fn_x4
E5M2X4 = mybir.dt.float8_e5m2_x4
E2M1X4 = mybir.dt.float4_e2m1fn_x4
ACT = mybir.ActivationFunctionType
ALU = mybir.AluOpType

P = 128
T = 4
STATE_LOADS = ((0, 1), (1, 1), (2, 2), (4, 2), (6, 2))
RUN = 2
KG = K // 512
FG = F // 512
HALF = 512
NH = M // HALF
MT = HALF // P


def tile_doremi_domain_reweighting_s9_kernel(
    tc, state, w_words, w_scales, ref_loss, member, alpha, out
):
    nc = tc.nc
    with ExitStack() as ctx:
        keep = ctx.enter_context(tc.tile_pool(name="keep", bufs=1))
        stage = ctx.enter_context(tc.tile_pool(name="stage", bufs=4))
        psum = ctx.enter_context(tc.psum_pool(name="psum", bufs=1))

        ident = keep.tile([P, P], F32, name="ident")
        ws_raw = keep.tile([P, KG, F], U8, name="ws_raw", align_bytes=64)
        ws = keep.tile([P, KG, T, F // T], U8, name="ws", align_bytes=64)
        w_raw = keep.tile([P, KG, 2 * F], U8, name="w_raw", align_bytes=64)
        w = keep.tile([P, KG, T, 2 * F // T], U8, name="w", align_bytes=64)
        ref_rows = keep.tile([P, P], BF16, name="ref_rows")
        ref_wide = keep.tile([P, T, 4, 4, 8], BF16, name="ref_wide")
        row_mod = keep.tile([P, 4], F32, name="row_mod")
        row_div = keep.tile([P, FG], F32, name="row_div")
        minus = keep.tile([P, FG], BF16, name="minus")
        zeros = keep.tile([P, HALF], BF16, name="zeros")
        negref = keep.tile([P, T, FG], F32, name="negref")
        totals = [keep.tile([P, MT], F32, name="totals%d" % h) for h in range(NH)]
        inv = [keep.tile([P, MT], F32, name="inv%d" % h) for h in range(NH)]
        warm = keep.tile([P, 1], F32, name="warm")
        warm_out = keep.tile([P, 1], F32, name="warm_out")
        s_codes = [keep.tile([P, KG, HALF], U32, name="s_codes%d" % h, align_bytes=64) for h in range(NH)]
        s_scales = [keep.tile([P, KG, HALF], U8, name="s_scales%d" % h, align_bytes=64) for h in range(NH)]
        s_group = [keep.tile([P, KG, HALF, T], BF16, name="s_group%d" % h, align_bytes=64) for h in range(NH)]
        x_codes = [keep.tile([P, FG, HALF], U32, name="x_codes%d" % h, align_bytes=64) for h in range(NH)]
        x_scales = [keep.tile([P, FG, HALF], U8, name="x_scales%d" % h, align_bytes=64) for h in range(NH)]
        m_codes = keep.tile([P, FG, D], U32, name="m_codes", align_bytes=64)
        m_scales = keep.tile([P, FG, D], U8, name="m_scales", align_bytes=64)
        s_raw = [
            keep.tile([P, n, K], BF16, name="s_raw%d" % j) for j, (first, n) in enumerate(STATE_LOADS)
        ]
        m_raw = [keep.tile([P, T, D], BF16, name="m_raw%d" % g) for g in range(FG)]
        al = [keep.tile([P, MT, D], BF16, name="al%d" % h) for h in range(NH)]

        def view(ap, pattern, **kw):
            return ap.rearrange(pattern, **kw)

        with tc.manual_schedule():
            nc.gpsimd.memset(ws_raw[:, 1, :].bitcast(I32), 0)
            nc.vector.memset(ws_raw[:, 0, :].bitcast(I32), 0)
            nc.vector.memset(ref_rows[:].bitcast(I32), 0)
            nc.vector.memset(zeros[:].bitcast(I32), 0)
            nc.vector.memset(warm[:], 0.0)
            make_identity(nc, ident[:])

            def load_state(j):
                first, n = STATE_LOADS[j]
                nc.sync.dma_start(
                    out=s_raw[j][:],
                    in_=view(state[first * P : (first + n) * P, :], "(i p) k -> p i k", p=P),
                )

            w_view = view(w_words, "g p n -> p g n")

            def load_w(a, b):
                nc.sync.dma_start(out=w_raw[:, :, a:b].bitcast(I32), in_=w_view[:, :, a:b].bitcast(I32))

            def load_scales(q):
                nc.sync.dma_start(
                    out=ws_raw[32 * q : 32 * q + 4, :, :].bitcast(I32),
                    in_=view(w_scales[:, 4 * q : 4 * q + 4, :], "g r n -> r g n").bitcast(I32),
                )

            m_view = view(member, "(g b t r) d -> g t b r d", b=16, t=T, r=8)

            def load_member(g):
                for t in range(T):
                    nc.sync.dma_start(out=m_raw[g][:, t, :], in_=m_view[g, t])

            a_view = view(alpha, "(h i p) d -> h p i d", i=MT, p=P)

            def load_alpha(h):
                nc.sync.dma_start(out=al[h][:], in_=a_view[h])

            nc.scalar.activation(out=warm_out[:], in_=warm[:], func=ACT.Exp)
            load_state(0)
            load_state(1)
            for q in range(4):
                load_scales(q)
            nc.sync.dma_start(out=ref_rows[0 : F // P, :], in_=view(ref_loss, "(c j) -> c j", j=P))
            load_state(2)
            load_w(0, 1024)
            load_w(1024, 4096)
            load_member(0)
            for j in range(3, 5):
                load_state(j)
            for g in range(1, FG):
                load_member(g)
            for h in range(NH):
                load_alpha(h)

            def dummy(n):
                for j in range(n):
                    junk = psum.tile([P, HALF], F32, name="junk", tag="A3")
                    nc.tensor.matmul(out=junk[:], lhsT=zeros[:, 0:P], rhs=zeros[:], start=True, stop=True)

            def turn_state(c, bank):
                xt = psum.tile([P, KG, 2, P], F32, name="xt%d" % c, tag=bank)
                j = max(j for j in range(len(STATE_LOADS)) if STATE_LOADS[j][0] <= c)
                words = s_raw[j][:, c - STATE_LOADS[j][0], :].bitcast(F32)
                for g in range(KG):
                    for u in range(2):
                        nc.tensor.transpose(
                            xt[:, g, u, :], words[:, 256 * g + u : 256 * (g + 1) : 2], ident[:]
                        )
                return xt

            def copy_state(c, xt, eng):
                h, i = divmod(c, MT)
                dst = s_group[h][:].bitcast(F32)[:, :, i * P : (i + 1) * P, :]
                src = view(xt[:], "p g u m -> p g m u")
                if eng == "v":
                    nc.vector.tensor_copy(out=dst, in_=src)
                else:
                    nc.scalar.copy(out=dst, in_=src)

            def quant_state(h, g, a, b):
                nc.vector.quantize_mx(
                    out=s_codes[h][:, g, a:b].bitcast(E4M3X4),
                    scales=s_scales[h][:, g, a:b],
                    in_=view(s_group[h][:, g, a:b, :], "p m t -> p (m t)"),
                )

            def perm_w(g, a, b):
                nc.vector.tensor_copy(
                    out=view(w[:, g, :, 256 * a : 256 * b].bitcast(I32), "p t (b w) -> p t b w", w=4),
                    in_=view(w_raw[:, g, 1024 * a : 1024 * b].bitcast(I32), "p (b t w) -> p t b w", t=T, w=4),
                )

            def perm_scales(g, a, b):
                nc.vector.tensor_copy(
                    out=view(ws[:, g, :, P * a : P * b].bitcast(I32), "p t (b w) -> p t b w", w=2),
                    in_=view(ws_raw[:, g, 512 * a : 512 * b].bitcast(I32), "p (b t w) -> p t b w", t=T, w=2),
                )

            def stage1(h, g2, t):
                bank = psum.tile([P, HALF], F32, name="loss_%d_%d_%d" % (h, g2, t), tag="A%d" % t)
                for g in range(KG):
                    nc.tensor.matmul_mx(
                        out=bank[:],
                        lhsT=w[:, g, t, 256 * g2 : 256 * (g2 + 1)].bitcast(E2M1X4),
                        lhsT_scale=ws[:, g, t, P * g2 : P * (g2 + 1)],
                        rhs=s_codes[h][:, g, :].bitcast(E4M3X4),
                        rhs_scale=s_scales[h][:, g, :],
                        start=(g == 0),
                        stop=(g == KG - 1),
                    )
                return bank

            def stage1_slice(h, g2, i):
                bank = psum.tile([P, T, P], F32, name="slice_%d_%d_%d" % (h, g2, i), tag="A%d" % i)
                for t in range(T):
                    for g in range(KG):
                        nc.tensor.matmul_mx(
                            out=bank[:, t, :],
                            lhsT=w[:, g, t, 256 * g2 : 256 * (g2 + 1)].bitcast(E2M1X4),
                            lhsT_scale=ws[:, g, t, P * g2 : P * (g2 + 1)],
                            rhs=s_codes[h][:, g, i * P : (i + 1) * P].bitcast(E4M3X4),
                            rhs_scale=s_scales[h][:, g, i * P : (i + 1) * P],
                            start=(g == 0),
                            stop=(g == KG - 1),
                        )
                return bank

            def evac_slice(e, bank, g2, i):
                for t in range(T):
                    nc.scalar.activation(
                        out=e[:, t, i * P : (i + 1) * P], in_=bank[:, t, :], func=ACT.Relu,
                        bias=negref[:, t, g2 : g2 + 1], scale=1.0,
                    )

            def evac(e, bank, g2, t, eng):
                if eng == "s":
                    nc.scalar.activation(
                        out=e[:, t, :], in_=bank[:], func=ACT.Relu, bias=negref[:, t, g2 : g2 + 1], scale=1.0
                    )
                else:
                    nc.vector.tensor_scalar(
                        out=e[:, t, :], in0=bank[:], scalar1=negref[:, t, g2 : g2 + 1], scalar2=0.0,
                        op0=ALU.add, op1=ALU.max,
                    )

            def weave(dst, src, a, b):
                nc.vector.tensor_copy(
                    out=view(dst[:, a:b, :], "p (c i) t -> p c t i", i=RUN),
                    in_=view(src[:, :, a:b], "p t (c i) -> p c t i", i=RUN),
                )

            def weave_s(dst, src, a, b):
                nc.scalar.copy(
                    out=view(dst[:, a:b, :], "p (c i) t -> p c t i", i=RUN),
                    in_=view(src[:, :, a:b], "p t (c i) -> p c t i", i=RUN),
                )

            def quant_x(h, g2, x, a, b):
                nc.vector.quantize_mx(
                    out=x_codes[h][:, g2, a:b].bitcast(E5M2X4),
                    scales=x_scales[h][:, g2, a:b],
                    in_=view(x[:, a:b, :], "p m t -> p (m t)"),
                )

            def quant_m(g2, x):
                nc.vector.quantize_mx(
                    out=m_codes[:, g2, :].bitcast(E4M3X4),
                    scales=m_scales[:, g2, :],
                    in_=view(x[:], "p m t -> p (m t)"),
                )

            def stage2(bank, h, i, g2):
                nc.tensor.matmul_mx(
                    out=bank[:],
                    lhsT=x_codes[h][:, g2, i * P : (i + 1) * P].bitcast(E5M2X4),
                    lhsT_scale=x_scales[h][:, g2, i * P : (i + 1) * P],
                    rhs=m_codes[:, g2, :].bitcast(E4M3X4),
                    rhs_scale=m_scales[:, g2, :],
                    start=(g2 == 0),
                    stop=(g2 == FG - 1),
                )

            def epi_exp(bank, h, i):
                e = stage.tile([P, D], F32, name="e_%d_%d" % (h, i), tag="e", bufs=8)
                nc.scalar.activation(out=e[:], in_=bank[:], func=ACT.Exp)
                return e

            def epi_mul(e, h, i):
                grown = stage.tile([P, D], F32, name="grown_%d_%d" % (h, i), tag="grown", bufs=8)
                nc.vector.scalar_tensor_tensor(
                    out=grown[:], in0=e[:], scalar=1.0, in1=al[h][:, i, :], op0=ALU.mult, op1=ALU.mult,
                    accum_out=totals[h][:, i : i + 1],
                )
                return grown

            def means(h, a, b):
                nc.vector.tensor_scalar(
                    out=totals[h][:, a:b], in0=totals[h][:, a:b], scalar1=1.0 / D, scalar2=None, op0=ALU.mult
                )

            def invert(h, a, b):
                nc.vector.reciprocal(out=inv[h][:, a:b], in_=totals[h][:, a:b])

            def fin(h, i, eng):
                res = stage.tile([P, D], F32, name="res_%d_%d" % (h, i), tag="res", bufs=8)
                scale = inv[h][:, i : i + 1]
                if eng == "s":
                    nc.scalar.activation(out=res[:], in_=done[h, i][:], func=ACT.Copy, scale=scale)
                elif eng == "v2":
                    nc.vector.tensor_scalar(
                        out=res[:], in0=done[h, i][:], scalar1=scale, scalar2=float(D), op0=ALU.mult, op1=ALU.mult
                    )
                else:
                    nc.vector.tensor_scalar(
                        out=res[:], in0=done[h, i][:], scalar1=scale, scalar2=None, op0=ALU.mult
                    )
                row = h * HALF + i * P
                nc.sync.dma_start(out=out[row : row + P, :], in_=res[:])

            done = {}
            es = {}
            exc = {}
            xs = {}
            mx = {}

            def run_stage1(h, g2, engs="ssss"):
                e = stage.tile([P, T, HALF], BF16, name="e_in_%d_%d" % (h, g2), tag="exc", bufs=5)
                for t in range(T):
                    bank = stage1(h, g2, t)
                    evac(e, bank, g2, t, engs[t])
                exc[h, g2] = e

            def weave_x(h, g2):
                x = stage.tile([P, HALF, T], BF16, name="x_%d_%d" % (h, g2), tag="x", bufs=3, align_bytes=64)
                weave(x, exc[h, g2], 0, HALF)
                xs[h, g2] = x

            def new_m(g2):
                mx[g2] = stage.tile([P, D, T], BF16, name="mx_%d" % g2, tag="mx", bufs=3, align_bytes=64)

            def weave_m(g2, a=0, b=D):
                weave(mx[g2], m_raw[g2], a, b)

            def qx(h, g2):
                quant_x(h, g2, xs[h, g2], 0, HALF)

            def qm(g2):
                quant_m(g2, mx[g2])

            lam = {}

            def run_stage2(h, i, groups):
                if (h, i) not in lam:
                    lam[h, i] = psum.tile([P, D], F32, name="lam_%d_%d" % (h, i), tag="B%d" % i)
                for g2 in groups:
                    stage2(lam[h, i], h, i, g2)

            def stage2_all(h, groups):
                for i in range(MT):
                    run_stage2(h, i, groups)

            def exp(h, i):
                es[h, i] = epi_exp(lam[h, i], h, i)

            def mul(h, i):
                done[h, i] = epi_mul(es[h, i], h, i)

            def new_exc(h, g2):
                exc[h, g2] = stage.tile([P, T, HALF], BF16, name="e_in_%d_%d" % (h, g2), tag="exc", bufs=5)

            def qs(i):
                for g in range(KG):
                    quant_state(0, g, P * i, P * (i + 1))

            def slice0(i):
                bank = stage1_slice(0, 0, i)
                evac_slice(exc[0, 0], bank, 0, i)

            def slice1(i):
                bank = stage1_slice(1, 3, i)
                evac_slice(exc[1, 3], bank, 3, i)

            dummy(5)
            nc.vector.tensor_reduce(
                out=row_mod[:], in_=view(ident[:, 0:16], "p (a q) -> p q a", q=4), axis=mybir.AxisListType.X, op=ALU.add
            )
            nc.vector.tensor_reduce(
                out=row_div[:], in_=view(ident[:, 0:16], "p (a q) -> p a q", q=4), axis=mybir.AxisListType.X, op=ALU.add
            )
            nc.vector.tensor_scalar(out=minus[:], in0=row_div[:], scalar1=-1.0, scalar2=None, op0=ALU.mult)
            for q in range(4):
                nc.vector.tensor_scalar(
                    out=ref_wide[:, :, q, :, :], in0=view(ref_rows[:], "p (j t r) -> p t j r", j=4, t=T),
                    scalar1=row_mod[:, q : q + 1], scalar2=None, op0=ALU.mult,
                )
            xt = [None] * (2 * MT)
            new_exc(0, 0)
            xt[0] = turn_state(0, "B0")
            copy_state(0, xt[0], "v")
            xt[1] = turn_state(1, "B1")
            refT = psum.tile([P, T, FG], F32, name="refT", tag="A3")
            for t in range(T):
                nc.tensor.matmul(
                    out=refT[:, t, :], lhsT=view(ref_wide[:, t, :, :, :], "p q j r -> p (q j r)"), rhs=minus[:],
                    start=True, stop=True,
                )
            copy_state(1, xt[1], "s")
            nc.scalar.copy(out=negref[:], in_=refT[:])
            for g in range(KG):
                perm_scales(g, 0, 1)
            qs(0)
            qs(1)
            xt[2] = turn_state(2, "B2")
            copy_state(2, xt[2], "s")
            for g in range(KG):
                perm_w(g, 0, 1)
            xt[3] = turn_state(3, "B3")
            copy_state(3, xt[3], "s")
            slice0(0)
            slice0(1)
            qs(2)
            qs(3)
            slice0(2)
            slice0(3)
            for g in range(KG):
                perm_w(g, 1, FG)
            for g in range(KG):
                perm_scales(g, 1, FG)
            run_stage1(0, 1)
            for c in range(MT, 2 * MT):
                xt[c] = turn_state(c, "B%d" % (c - MT))
                copy_state(c, xt[c], "s")
            run_stage1(0, 2)
            run_stage1(0, 3)
            for g2 in range(FG):
                new_m(g2)
            weave_m(0)
            weave_x(0, 0)
            qm(0)
            qx(0, 0)
            stage2_all(0, [0])
            weave_x(0, 1)
            weave_m(1)
            qx(0, 1)
            for g in range(KG):
                quant_state(1, g, 0, 512)
            qm(1)
            run_stage1(1, 0)
            stage2_all(0, [1])
            weave_x(0, 2)
            weave_m(2)
            qx(0, 2)
            qm(2)
            run_stage1(1, 1)
            stage2_all(0, [2])
            weave_x(0, 3)
            weave_m(3)
            qx(0, 3)
            qm(3)
            run_stage1(1, 2)
            stage2_all(0, [3])
            weave_x(1, 0)
            weave_x(1, 1)
            qx(1, 0)
            qx(1, 1)
            for i in range(MT):
                exp(0, i)
            run_stage1(1, 3)
            weave_x(1, 2)
            mul(0, 0)
            qx(1, 2)
            mul(0, 1)
            mul(0, 2)
            means(0, 0, 2)
            mul(0, 3)
            invert(0, 0, 2)
            means(0, 2, 4)
            x = stage.tile([P, HALF, T], BF16, name="x_1_3", tag="x", bufs=3, align_bytes=64)
            last = exc[1, 3]
            stage2_all(1, [0, 1, 2])

            def piece(i):
                weave(x, last, i * P, (i + 1) * P)

            def qpiece(i):
                quant_x(1, 3, x, i * P, (i + 1) * P)

            piece(0)
            invert(0, 2, 4)
            piece(1)
            qpiece(0)
            fin(0, 0, "s")
            fin(0, 1, "s")
            piece(2)
            qpiece(1)
            piece(3)
            qpiece(2)
            qpiece(3)
            fin(0, 2, "v")
            fin(0, 3, "v")
            for i in range(MT):
                run_stage2(1, i, [3])
                exp(1, i)
            mul(1, 0)
            mul(1, 1)
            means(1, 0, 2)
            mul(1, 2)
            invert(1, 0, 2)
            mul(1, 3)
            fin(1, 0, "s")
            fin(1, 1, "s")
            invert(1, 2, 4)
            fin(1, 2, "v2")
            fin(1, 3, "v2")
